import numpy as np
import ml_dtypes


def mxq(x, axis, fmt="e4m3"):
    dtype, down = {"e4m3": (ml_dtypes.float8_e4m3fn, 7), "e5m2": (ml_dtypes.float8_e5m2, 14)}[fmt]
    v = np.moveaxis(np.asarray(x, np.float32).astype(ml_dtypes.bfloat16).astype(np.float64), axis, -1)
    blocks = v.reshape(v.shape[:-1] + (-1, 32))
    amax = np.abs(blocks).max(-1, keepdims=True)
    byte = np.maximum(np.where(amax > 0, np.frexp(amax)[1] - 1 + 127, 0) - down, 1)
    scale = np.exp2(byte - 127.0)
    codes = (blocks / scale).astype(np.float32).astype(dtype).astype(np.float64)
    return np.moveaxis((codes * scale).reshape(v.shape), -1, axis)


WIDE = False


def mx_kscale(k):
    if not WIDE:
        return np.ones(k)
    levels = np.array([30, -30])
    if k % 512:
        return np.exp2(np.random.permutation(np.resize(levels, k // 32))).repeat(32)
    a = np.empty((k // 512, 16))
    for p in range(k // 512):
        a[p, :8] = np.random.permutation(np.resize(levels, 8))
        for g in range(8):
            far = levels[np.abs(levels - a[p, g]) >= 10]
            a[p, g + 8] = far[np.random.randint(len(far))]
    return np.exp2(a.ravel()).repeat(32)


def f64(x):
    return np.asarray(x).astype(np.float64)


def striped(idx):
    return np.tile(np.asarray(idx).reshape(-1, 16).T, (8, 1)).astype(np.uint16)


def unstriped(offs):
    return offs[:16].T.reshape(-1).astype(np.int64)


E2M1 = np.array([0.0, 0.5, 1.0, 1.5, 2.0, 3.0, 4.0, 6.0, -0.0, -0.5, -1.0, -1.5, -2.0, -3.0, -4.0, -6.0])


def pack_weight(w, fmt):
    k, n = w.shape
    w = f64(np.asarray(w, np.float32).astype(ml_dtypes.bfloat16)).reshape(k // 32, 32, n)
    amax = np.abs(w).max(1)
    if fmt in ("e4m3", "e5m2"):
        byte = np.frexp(amax)[1] - 1 + 127 - (7 if fmt == "e4m3" else 14)
    else:
        mant, ex = np.frexp(amax / 6.0)
        byte = np.where(mant > 0.5, ex, ex - 1) + 127
    byte = np.clip(np.where(amax > 0, byte, 1), 1, 254)
    scaled = (w * np.exp2(127.0 - byte)[:, None, :]).reshape(k, n).astype(np.float32)
    by_word = np.ascontiguousarray(scaled.reshape(k // 512, 128, 4, n).transpose(0, 1, 3, 2))
    if fmt in ("e4m3", "e5m2"):
        words = by_word.astype(ml_dtypes.float8_e4m3fn if fmt == "e4m3" else ml_dtypes.float8_e5m2).view(np.uint8)
    else:
        c = by_word.astype(ml_dtypes.float4_e2m1fn).view(np.uint8) & 0xF
        words = (c[..., 0::2] | (c[..., 1::2] << 4)).reshape(k // 512, 128, 2 * n)
    return np.ascontiguousarray(words), np.ascontiguousarray(byte.astype(np.uint8).reshape(k // 512, 16, n))


def unpack_weight(words, scales, fmt):
    g, _, n = scales.shape
    words = np.ascontiguousarray(words).reshape(g, 128, n, -1)
    if fmt in ("e4m3", "e5m2"):
        vals = words.view(ml_dtypes.float8_e4m3fn if fmt == "e4m3" else ml_dtypes.float8_e5m2).astype(np.float64)
    else:
        nib = np.empty((g, 128, n, 4), np.uint8)
        nib[..., 0::2] = words & 0xF
        nib[..., 1::2] = words >> 4
        vals = E2M1[nib]
    vals = vals * np.repeat(np.exp2(scales.astype(np.float64) - 127.0), 8, axis=1)[..., None]
    return vals.transpose(0, 1, 3, 2).reshape(g * 512, n)


def e4m3fn_bytes(y):
    return np.clip(np.asarray(y, np.float64), -448.0, 448.0).astype(np.float32).astype(ml_dtypes.float8_e4m3fn).view(np.uint8)


def e4m3fn_values(b):
    return np.asarray(b, np.uint8).view(ml_dtypes.float8_e4m3fn).astype(np.float64)


K, T, J, R, U, V, E, N = 512, 1024, 256, 512, 128, 1024, 512, 256


def setup_inputs():
    n = np.random.standard_normal
    idx = np.random.permutation(T)[:J]
    idx2 = np.random.permutation(J)[:U]
    idx3 = np.random.permutation(V)[:U]
    idx4 = np.random.permutation(E)[:U]
    fk = mx_kscale(K)
    fr = mx_kscale(R)
    xtp = pack_weight(n((K, T)) / fk[:, None], "e5m2")
    wp = pack_weight(n((K, R)) * 1 / np.sqrt(K) * fk[:, None] * fr, "e2m1")
    w2p = pack_weight(n((K, R)) * 1 / np.sqrt(K) * fk[:, None] * fr, "e4m3")
    wbp = pack_weight(n((R, N)) * 1 / np.sqrt(R) / fr[:, None], "e2m1")
    return {
        "xt_words": xtp[0],
        "xt_scales": xtp[1],
        "w_words": wp[0],
        "w_scales": wp[1],
        "w2_words": w2p[0],
        "w2_scales": w2p[1],
        "wb_words": wbp[0],
        "wb_scales": wbp[1],
        "ca": e4m3fn_bytes(60.0 * n((N, V))),
        "sz": (np.random.uniform(0.004, 0.012, (N, 1))).astype(np.float32),
        "offs": striped(idx),
        "offs2": striped(idx2),
        "offs3": striped(idx3),
        "offs4": striped(idx4),
    }


def reference(xt_words, xt_scales, w_words, w_scales, w2_words, w2_scales, wb_words, wb_scales, ca, sz, offs, offs2, offs3, offs4):
    idx = unstriped(offs)
    idx2 = unstriped(offs2)
    idx3 = unstriped(offs3)
    idx4 = unstriped(offs4)
    xtu = unpack_weight(xt_words, xt_scales, "e5m2")
    wu = unpack_weight(w_words, w_scales, "e2m1")
    w2u = unpack_weight(w2_words, w2_scales, "e4m3")
    wbu = unpack_weight(wb_words, wb_scales, "e2m1")
    xtidxg = xtu[:, idx]
    a = wu.T @ xtidxg
    b = w2u.T @ xtidxg
    hid = np.maximum(a, b)
    hidq = mxq(hid, 0, "e4m3")
    p = wbu.T @ hidq
    g1 = e4m3fn_values(ca)[:, idx3] * f64(sz)
    m0 = p[:, idx2] * g1
    y = np.zeros((N, E))
    y[:, idx4] = m0
    return y

@@ -1,0 +1,158 @@
+from contextlib import ExitStack
+
+import concourse.mybir as mybir
+
+K, T, J, R, U, V, E, N = 512, 1024, 256, 512, 128, 1024, 512, 256
+FLOPS = 2 * K * R * J * 2 + 2 * R * N * J
+
+F32 = mybir.dt.float32
+BF16 = mybir.dt.bfloat16
+I32 = mybir.dt.int32
+U32 = mybir.dt.uint32
+U16 = mybir.dt.uint16
+U8 = mybir.dt.uint8
+FP8 = mybir.dt.float8_e4m3fn
+E4M3X4 = mybir.dt.float8_e4m3fn_x4
+E5M2X4 = mybir.dt.float8_e5m2_x4
+E2M1X4 = mybir.dt.float4_e2m1fn_x4
+ALU = mybir.AluOpType
+COPY = mybir.ActivationFunctionType.Copy
+
+P = 128
+PACK = 4
+HALF = 128
+
+
+def tile_list_outcomegain_kernel(tc, xt_words, xt_scales, w_words, w_scales, w2_words, w2_scales,
+                                     wb_words, wb_scales, ca, sz, offs, offs2, offs3, offs4, out):
+    nc = tc.nc
+    with ExitStack() as ctx:
+        sb = ctx.enter_context(tc.tile_pool(name="sb", bufs=1))
+        ps = ctx.enter_context(tc.psum_pool(name="ps", bufs=1))
+
+        def tile(name, shape, dtype):
+            return sb.tile(shape, dtype, name=name, align_bytes=64)
+
+        l1 = tile("l1", [P, J // 16], U16)
+        l2 = tile("l2", [P, U // 16], U16)
+        l3 = tile("l3", [P, U // 16], U16)
+        l4 = tile("l4", [P, U // 16], U16)
+        xw = tile("xw", [P, T], U32)
+        xs = tile("xs", [P, T], U8)
+        w_raw = tile("w_raw", [P, 2 * R], U8)
+        ws_raw = tile("ws_raw", [P, 4 * R], U8)
+        w2_raw = tile("w2_raw", [P, R], U32)
+        w2s_raw = tile("w2s_raw", [P, 2 * R], U8)
+        wb = tile("wb", [P, 2 * N], U8)
+        wbs = tile("wbs", [P, N], U8)
+        cat = [tile(f"cat{n}", [P, V], U8) for n in range(2)]
+        step = tile("step", [P, 2, 1], F32)
+        page = [tile(f"page{n}", [P, E], F32) for n in range(2)]
+
+        nc.vector.memset(ws_raw[:, 0:R].bitcast(I32), 0)
+        nc.vector.memset(xs[:].bitcast(I32), 0)
+        nc.vector.memset(w2s_raw[0:64, :].bitcast(I32), 0)
+        nc.vector.memset(wbs[:].bitcast(I32), 0)
+        for n in range(2):
+            nc.vector.memset(page[n][:], 0.0)
+
+        def load_rows(queue, plane, scales, q):
+            queue.dma_start(out=plane[32 * q : 32 * q + 4, :].bitcast(I32),
+                            in_=scales[0].bitcast(I32)[4 * q : 4 * q + 4, :])
+
+        nc.scalar.dma_start(out=w_raw[:].bitcast(I32), in_=w_words[0].bitcast(I32))
+        nc.sync.dma_start(l1[:], offs)
+        nc.scalar.dma_start(out=ws_raw[0:4, :].bitcast(I32).rearrange("p (q c) -> p q c", q=4),
+                            in_=w_scales[0].bitcast(I32).rearrange("(q r) c -> r q c", q=4))
+        for q in range(3):
+            load_rows(nc.sync, xs, xt_scales, q)
+        load_rows(nc.scalar, xs, xt_scales, 3)
+        nc.scalar.dma_start(out=xw[:].bitcast(I32), in_=xt_words[0].rearrange("p n t -> p (n t)").bitcast(I32))
+        nc.sync.dma_start(out=w2_raw[:].bitcast(I32), in_=w2_words[0].rearrange("p n t -> p (n t)").bitcast(I32))
+        w2s_rows = w2_scales[0].bitcast(I32).rearrange("(h q r) c -> q r h c", h=2, q=2)
+        for q in range(2):
+            nc.sync.dma_start(out=w2s_raw[32 * q : 32 * q + 4, :].bitcast(I32).rearrange("p (h c) -> p h c", h=2),
+                              in_=w2s_rows[q])
+        nc.sync.dma_start(l3[:], offs3)
+        for n in range(2):
+            nc.sync.dma_start(out=cat[n][:], in_=ca[P * n : P * (n + 1), :])
+        with nc.allow_non_contiguous_dma(reason="one step a partition for each half of the output features"):
+            nc.sync.dma_start(out=step[:], in_=sz.rearrange("(h p) o -> p h o", p=P))
+        nc.sync.dma_start(out=wb[:].bitcast(I32), in_=wb_words[0].bitcast(I32))
+        for q in range(4):
+            load_rows(nc.sync, wbs, wb_scales, q)
+        nc.sync.dma_start(l2[:], offs2)
+        nc.sync.dma_start(l4[:], offs4)
+
+        w_t = [tile(f"w_t{t}", [P, 2 * P], U8) for t in range(PACK)]
+        w2_t = [tile(f"w2_t{t}", [P, P], U32) for t in range(PACK)]
+        ws = tile("ws", [P, R], U8)
+        w2s = tile("w2s", [P, R], U8)
+        xg = [tile(f"xg{h}", [P, HALF], U32) for h in range(2)]
+        xsg = [tile(f"xsg{h}", [P, HALF], U8) for h in range(2)]
+
+        for q in range(1, 4):
+            nc.vector.tensor_copy(out=ws_raw[32 * q : 32 * q + 4, 0:R].bitcast(I32),
+                                  in_=ws_raw[0:4, R * q : R * (q + 1)].bitcast(I32))
+        nc.vector.tensor_copy(out=xsg[0][:], in_=xs[:].indirect(l1[:, 0:8]))
+        nc.vector.tensor_copy(out=ws[:].rearrange("p (t m) -> p t m", t=PACK),
+                              in_=ws_raw[:, 0:R].rearrange("p (m t) -> p t m", t=PACK))
+        for t in range(PACK):
+            nc.scalar.copy(out=w_t[t][:].bitcast(U16), in_=w_raw[:].bitcast(U16)[:, t : R : PACK])
+        nc.vector.tensor_copy(out=xg[0][:], in_=xw[:].indirect(l1[:, 0:8]))
+        nc.vector.tensor_copy(out=xsg[1][:], in_=xs[:].indirect(l1[:, 8:16]))
+        nc.vector.tensor_copy(out=xg[1][:], in_=xw[:].indirect(l1[:, 8:16]))
+        nc.vector.tensor_copy(out=w2s_raw[64:128, 0:R].bitcast(I32), in_=w2s_raw[0:64, R : 2 * R].bitcast(I32))
+        nc.vector.tensor_copy(out=w2s[:].rearrange("p (t m) -> p t m", t=PACK),
+                              in_=w2s_raw[:, 0:R].rearrange("p (m t) -> p t m", t=PACK))
+        for t in range(PACK):
+            nc.scalar.copy(out=w2_t[t][:], in_=w2_raw[:, t : R : PACK])
+
+        pa = [ps.tile([P, PACK, HALF], F32, name=f"pa{h}") for h in range(2)]
+        pb = [ps.tile([P, PACK, HALF], F32, name=f"pb{h}") for h in range(2)]
+        pp = [[ps.tile([P, HALF], F32, name=f"pp{n}{h}") for h in range(2)] for n in range(2)]
+        a_sb = [tile(f"a_sb{h}", [P, HALF, PACK], F32) for h in range(2)]
+        for h in range(2):
+            for t in range(PACK):
+                nc.tensor.matmul_mx(out=pa[h][:, t, :], lhsT=w_t[t][:].bitcast(E2M1X4),
+                                    lhsT_scale=ws[:, P * t : P * (t + 1)],
+                                    rhs=xg[h][:].bitcast(E5M2X4), rhs_scale=xsg[h][:], start=True, stop=True)
+            nc.scalar.copy(out=a_sb[h][:], in_=pa[h][:].rearrange("p t j -> p j t"))
+        for h in range(2):
+            for t in range(PACK):
+                nc.tensor.matmul_mx(out=pb[h][:, t, :], lhsT=w2_t[t][:].bitcast(E4M3X4),
+                                    lhsT_scale=w2s[:, P * t : P * (t + 1)],
+                                    rhs=xg[h][:].bitcast(E5M2X4), rhs_scale=xsg[h][:], start=True, stop=True)
+
+        cg = [tile(f"cg{n}", [P, U], U8) for n in range(2)]
+        gain = [tile(f"gain{n}", [P, U], F32) for n in range(2)]
+        for n in range(2):
+            nc.vector.tensor_copy(out=cg[n][:], in_=cat[n][:].indirect(l3[:]))
+            nc.scalar.activation(out=gain[n][:], in_=cg[n][:].bitcast(FP8), func=COPY, scale=step[:, n, :])
+
+        hid = [tile(f"hid{h}", [P, HALF, PACK], BF16) for h in range(2)]
+        hq = [tile(f"hq{h}", [P, HALF], U32) for h in range(2)]
+        hs = [tile(f"hs{h}", [P, HALF], U8) for h in range(2)]
+        p_sb = [tile(f"p_sb{n}", [P, J], F32) for n in range(2)]
+        for h in range(2):
+            nc.vector.tensor_tensor(out=hid[h][:], in0=pb[h][:].rearrange("p t j -> p j t"), in1=a_sb[h][:], op=ALU.max)
+            nc.vector.quantize_mx(out=hq[h][:].bitcast(E4M3X4), scales=hs[h][:],
+                                  in_=hid[h][:].rearrange("p j t -> p (j t)"))
+            for n in range(2):
+                nc.tensor.matmul_mx(out=pp[n][h][:], lhsT=wb[:, 2 * P * n : 2 * P * (n + 1)].bitcast(E2M1X4),
+                                    lhsT_scale=wbs[:, P * n : P * (n + 1)],
+                                    rhs=hq[h][:].bitcast(E4M3X4), rhs_scale=hs[h][:], start=True, stop=True)
+                cols = slice(HALF * h, HALF * (h + 1))
+                if h == 1 and n == 1:
+                    nc.vector.tensor_copy(out=p_sb[n][:, cols], in_=pp[n][h][:])
+                else:
+                    nc.scalar.copy(out=p_sb[n][:, cols], in_=pp[n][h][:])
+
+        m0 = tile("m0", [P, U], F32)
+        picked = tile("picked", [P, U], F32)
+        nc.vector.tensor_tensor(out=m0[:], in0=p_sb[0][:].indirect(l2[:]), in1=gain[0][:], op=ALU.mult)
+        nc.scalar.activation(out=picked[:], in_=p_sb[1][:].indirect(l2[:]), func=COPY)
+        nc.scalar.activation(out=page[0][:].indirect(l4[:]), in_=m0[:], func=COPY)
+        nc.vector.tensor_tensor(out=page[1][:].indirect(l4[:]), in0=picked[:], in1=gain[1][:], op=ALU.mult)
+        nc.scalar.dma_start(out=out[0:P, :], in_=page[0][:])
+        nc.sync.dma_start(out=out[P : 2 * P, :], in_=page[1][:])

@@ -30,8 +30,8 @@ def tile_list_outcomegain_kernel(tc, xt_words, xt_scales, w_words, w_scales, w2_
         sb = ctx.enter_context(tc.tile_pool(name="sb", bufs=1))
         ps = ctx.enter_context(tc.psum_pool(name="ps", bufs=1))
 
-        def tile(name, shape, dtype):
-            return sb.tile(shape, dtype, name=name, align_bytes=64)
+        def tile(name, shape, dtype, tag=None):
+            return sb.tile(shape, dtype, name=name, tag=tag or name, align_bytes=64)
 
         l1 = tile("l1", [P, J // 16], U16)
         l2 = tile("l2", [P, U // 16], U16)
@@ -40,7 +40,7 @@ def tile_list_outcomegain_kernel(tc, xt_words, xt_scales, w_words, w_scales, w2_
         xw = tile("xw", [P, T], U32)
         xs = tile("xs", [P, T], U8)
         w_raw = tile("w_raw", [P, 2 * R], U8)
-        ws_raw = tile("ws_raw", [P, 4 * R], U8)
+        ws_raw = tile("ws_raw", [P, 2 * R], U8)
         w2_raw = tile("w2_raw", [P, R], U32)
         w2s_raw = tile("w2s_raw", [P, 2 * R], U8)
         wb = tile("wb", [P, 2 * N], U8)
@@ -49,8 +49,8 @@ def tile_list_outcomegain_kernel(tc, xt_words, xt_scales, w_words, w_scales, w2_
         step = tile("step", [P, 2, 1], F32)
         page = [tile(f"page{n}", [P, E], F32) for n in range(2)]
 
-        nc.vector.memset(ws_raw[:, 0:R].bitcast(I32), 0)
         nc.vector.memset(xs[:].bitcast(I32), 0)
+        nc.gpsimd.memset(ws_raw[0:64, :].bitcast(I32), 0)
         nc.vector.memset(w2s_raw[0:64, :].bitcast(I32), 0)
         nc.vector.memset(wbs[:].bitcast(I32), 0)
         for n in range(2):
@@ -60,27 +60,33 @@ def tile_list_outcomegain_kernel(tc, xt_words, xt_scales, w_words, w_scales, w2_
             queue.dma_start(out=plane[32 * q : 32 * q + 4, :].bitcast(I32),
                             in_=scales[0].bitcast(I32)[4 * q : 4 * q + 4, :])
 
-        nc.scalar.dma_start(out=w_raw[:].bitcast(I32), in_=w_words[0].bitcast(I32))
+        def load_folded(queue, plane, scales):
+            rows = scales[0].bitcast(I32).rearrange("(h q r) c -> q r h c", h=2, q=2)
+            for q in range(2):
+                queue.dma_start(out=plane[32 * q : 32 * q + 4, :].bitcast(I32).rearrange("p (h c) -> p h c", h=2),
+                                in_=rows[q])
+
+        def unfold_and_deal(dealt, plane):
+            nc.vector.tensor_copy(out=plane[64:128, 0:R].bitcast(I32), in_=plane[0:64, R : 2 * R].bitcast(I32))
+            nc.vector.tensor_copy(out=dealt[:].rearrange("p (t m) -> p t m", t=PACK),
+                                  in_=plane[:, 0:R].rearrange("p (m t) -> p t m", t=PACK))
+
+        nc.gpsimd.dma_start(out=w_raw[:].bitcast(I32), in_=w_words[0].bitcast(I32))
+        nc.gpsimd.dma_start(out=wb[:].bitcast(I32), in_=wb_words[0].bitcast(I32))
         nc.sync.dma_start(l1[:], offs)
-        nc.scalar.dma_start(out=ws_raw[0:4, :].bitcast(I32).rearrange("p (q c) -> p q c", q=4),
-                            in_=w_scales[0].bitcast(I32).rearrange("(q r) c -> r q c", q=4))
-        for q in range(3):
-            load_rows(nc.sync, xs, xt_scales, q)
-        load_rows(nc.scalar, xs, xt_scales, 3)
-        nc.scalar.dma_start(out=xw[:].bitcast(I32), in_=xt_words[0].rearrange("p n t -> p (n t)").bitcast(I32))
+        load_folded(nc.scalar, ws_raw, w_scales)
+        for q in range(4):
+            load_rows(nc.scalar if q < 2 else nc.sync, xs, xt_scales, q)
+        nc.sync.dma_start(out=xw[:].bitcast(I32), in_=xt_words[0].rearrange("p n t -> p (n t)").bitcast(I32))
         nc.sync.dma_start(out=w2_raw[:].bitcast(I32), in_=w2_words[0].rearrange("p n t -> p (n t)").bitcast(I32))
-        w2s_rows = w2_scales[0].bitcast(I32).rearrange("(h q r) c -> q r h c", h=2, q=2)
-        for q in range(2):
-            nc.sync.dma_start(out=w2s_raw[32 * q : 32 * q + 4, :].bitcast(I32).rearrange("p (h c) -> p h c", h=2),
-                              in_=w2s_rows[q])
+        load_folded(nc.sync, w2s_raw, w2_scales)
         nc.sync.dma_start(l3[:], offs3)
         for n in range(2):
             nc.sync.dma_start(out=cat[n][:], in_=ca[P * n : P * (n + 1), :])
-        with nc.allow_non_contiguous_dma(reason="one step a partition for each half of the output features"):
-            nc.sync.dma_start(out=step[:], in_=sz.rearrange("(h p) o -> p h o", p=P))
-        nc.sync.dma_start(out=wb[:].bitcast(I32), in_=wb_words[0].bitcast(I32))
         for q in range(4):
             load_rows(nc.sync, wbs, wb_scales, q)
+        with nc.allow_non_contiguous_dma(reason="one step a partition for each half of the output features"):
+            nc.sync.dma_start(out=step[:], in_=sz.rearrange("(h p) o -> p h o", p=P))
         nc.sync.dma_start(l2[:], offs2)
         nc.sync.dma_start(l4[:], offs4)
 
@@ -91,20 +97,14 @@ def tile_list_outcomegain_kernel(tc, xt_words, xt_scales, w_words, w_scales, w2_
         xg = [tile(f"xg{h}", [P, HALF], U32) for h in range(2)]
         xsg = [tile(f"xsg{h}", [P, HALF], U8) for h in range(2)]
 
-        for q in range(1, 4):
-            nc.vector.tensor_copy(out=ws_raw[32 * q : 32 * q + 4, 0:R].bitcast(I32),
-                                  in_=ws_raw[0:4, R * q : R * (q + 1)].bitcast(I32))
-        nc.vector.tensor_copy(out=xsg[0][:], in_=xs[:].indirect(l1[:, 0:8]))
-        nc.vector.tensor_copy(out=ws[:].rearrange("p (t m) -> p t m", t=PACK),
-                              in_=ws_raw[:, 0:R].rearrange("p (m t) -> p t m", t=PACK))
+        unfold_and_deal(ws, ws_raw)
         for t in range(PACK):
             nc.scalar.copy(out=w_t[t][:].bitcast(U16), in_=w_raw[:].bitcast(U16)[:, t : R : PACK])
-        nc.vector.tensor_copy(out=xg[0][:], in_=xw[:].indirect(l1[:, 0:8]))
-        nc.vector.tensor_copy(out=xsg[1][:], in_=xs[:].indirect(l1[:, 8:16]))
-        nc.vector.tensor_copy(out=xg[1][:], in_=xw[:].indirect(l1[:, 8:16]))
-        nc.vector.tensor_copy(out=w2s_raw[64:128, 0:R].bitcast(I32), in_=w2s_raw[0:64, R : 2 * R].bitcast(I32))
-        nc.vector.tensor_copy(out=w2s[:].rearrange("p (t m) -> p t m", t=PACK),
-                              in_=w2s_raw[:, 0:R].rearrange("p (m t) -> p t m", t=PACK))
+        for h in range(2):
+            nc.vector.tensor_copy(out=xsg[h][:], in_=xs[:].indirect(l1[:, 8 * h : 8 * h + 8]))
+        for h in range(2):
+            nc.vector.tensor_copy(out=xg[h][:], in_=xw[:].indirect(l1[:, 8 * h : 8 * h + 8]))
+        unfold_and_deal(w2s, w2s_raw)
         for t in range(PACK):
             nc.scalar.copy(out=w2_t[t][:], in_=w2_raw[:, t : R : PACK])
 
@@ -130,20 +130,20 @@ def tile_list_outcomegain_kernel(tc, xt_words, xt_scales, w_words, w_scales, w2_
             nc.vector.tensor_copy(out=cg[n][:], in_=cat[n][:].indirect(l3[:]))
             nc.scalar.activation(out=gain[n][:], in_=cg[n][:].bitcast(FP8), func=COPY, scale=step[:, n, :])
 
-        hid = [tile(f"hid{h}", [P, HALF, PACK], BF16) for h in range(2)]
+        hid = tile("hid", [P, 2, HALF, PACK], BF16, tag="cat1")
         hq = [tile(f"hq{h}", [P, HALF], U32) for h in range(2)]
         hs = [tile(f"hs{h}", [P, HALF], U8) for h in range(2)]
         p_sb = [tile(f"p_sb{n}", [P, J], F32) for n in range(2)]
         for h in range(2):
-            nc.vector.tensor_tensor(out=hid[h][:], in0=pb[h][:].rearrange("p t j -> p j t"), in1=a_sb[h][:], op=ALU.max)
+            nc.vector.tensor_tensor(out=hid[:, h], in0=pb[h][:].rearrange("p t j -> p j t"), in1=a_sb[h][:], op=ALU.max)
             nc.vector.quantize_mx(out=hq[h][:].bitcast(E4M3X4), scales=hs[h][:],
-                                  in_=hid[h][:].rearrange("p j t -> p (j t)"))
+                                  in_=hid[:, h].rearrange("p j t -> p (j t)"))
             for n in range(2):
                 nc.tensor.matmul_mx(out=pp[n][h][:], lhsT=wb[:, 2 * P * n : 2 * P * (n + 1)].bitcast(E2M1X4),
                                     lhsT_scale=wbs[:, P * n : P * (n + 1)],
                                     rhs=hq[h][:].bitcast(E4M3X4), rhs_scale=hs[h][:], start=True, stop=True)
                 cols = slice(HALF * h, HALF * (h + 1))
-                if h == 1 and n == 1:
+                if n == 1:
                     nc.vector.tensor_copy(out=p_sb[n][:, cols], in_=pp[n][h][:])
                 else:
                     nc.scalar.copy(out=p_sb[n][:, cols], in_=pp[n][h][:])

@@ -40,7 +40,8 @@ def tile_list_outcomegain_kernel(tc, xt_words, xt_scales, w_words, w_scales, w2_
         xw = tile("xw", [P, T], U32)
         xs = tile("xs", [P, T], U8)
         w_raw = tile("w_raw", [P, 2 * R], U8)
-        ws_raw = tile("ws_raw", [P, 2 * R], U8)
+        ws_stage = tile("ws_stage", [4, 4, R // 4], U32)
+        ws_raw = tile("ws_raw", [P, R], U8)
         w2_raw = tile("w2_raw", [P, R], U32)
         w2s_raw = tile("w2s_raw", [P, 2 * R], U8)
         wb = tile("wb", [P, 2 * N], U8)
@@ -50,7 +51,7 @@ def tile_list_outcomegain_kernel(tc, xt_words, xt_scales, w_words, w_scales, w2_
         page = [tile(f"page{n}", [P, E], F32) for n in range(2)]
 
         nc.vector.memset(xs[:].bitcast(I32), 0)
-        nc.gpsimd.memset(ws_raw[0:64, :].bitcast(I32), 0)
+        nc.vector.memset(ws_raw[:].bitcast(I32), 0)
         nc.vector.memset(w2s_raw[0:64, :].bitcast(I32), 0)
         nc.vector.memset(wbs[:].bitcast(I32), 0)
         for n in range(2):
@@ -66,15 +67,14 @@ def tile_list_outcomegain_kernel(tc, xt_words, xt_scales, w_words, w_scales, w2_
                 queue.dma_start(out=plane[32 * q : 32 * q + 4, :].bitcast(I32).rearrange("p (h c) -> p h c", h=2),
                                 in_=rows[q])
 
-        def unfold_and_deal(dealt, plane):
-            nc.vector.tensor_copy(out=plane[64:128, 0:R].bitcast(I32), in_=plane[0:64, R : 2 * R].bitcast(I32))
+        def deal(dealt, plane):
             nc.vector.tensor_copy(out=dealt[:].rearrange("p (t m) -> p t m", t=PACK),
                                   in_=plane[:, 0:R].rearrange("p (m t) -> p t m", t=PACK))
 
-        nc.gpsimd.dma_start(out=w_raw[:].bitcast(I32), in_=w_words[0].bitcast(I32))
-        nc.gpsimd.dma_start(out=wb[:].bitcast(I32), in_=wb_words[0].bitcast(I32))
         nc.sync.dma_start(l1[:], offs)
-        load_folded(nc.scalar, ws_raw, w_scales)
+        nc.scalar.dma_start(out=ws_stage[:].bitcast(I32),
+                            in_=w_scales[0].bitcast(I32).rearrange("(q r) c -> r q c", q=4))
+        nc.scalar.dma_start(out=w_raw[:].bitcast(I32), in_=w_words[0].bitcast(I32))
         for q in range(4):
             load_rows(nc.scalar if q < 2 else nc.sync, xs, xt_scales, q)
         nc.sync.dma_start(out=xw[:].bitcast(I32), in_=xt_words[0].rearrange("p n t -> p (n t)").bitcast(I32))
@@ -83,6 +83,7 @@ def tile_list_outcomegain_kernel(tc, xt_words, xt_scales, w_words, w_scales, w2_
         nc.sync.dma_start(l3[:], offs3)
         for n in range(2):
             nc.sync.dma_start(out=cat[n][:], in_=ca[P * n : P * (n + 1), :])
+        nc.sync.dma_start(out=wb[:].bitcast(I32), in_=wb_words[0].bitcast(I32))
         for q in range(4):
             load_rows(nc.sync, wbs, wb_scales, q)
         with nc.allow_non_contiguous_dma(reason="one step a partition for each half of the output features"):
@@ -97,27 +98,30 @@ def tile_list_outcomegain_kernel(tc, xt_words, xt_scales, w_words, w_scales, w2_
         xg = [tile(f"xg{h}", [P, HALF], U32) for h in range(2)]
         xsg = [tile(f"xsg{h}", [P, HALF], U8) for h in range(2)]
 
-        unfold_and_deal(ws, ws_raw)
+        for q in range(4):
+            nc.vector.tensor_copy(out=ws_raw[32 * q : 32 * q + 4, :].bitcast(U32), in_=ws_stage[:, q, :])
+        deal(ws, ws_raw)
         for t in range(PACK):
             nc.scalar.copy(out=w_t[t][:].bitcast(U16), in_=w_raw[:].bitcast(U16)[:, t : R : PACK])
         for h in range(2):
             nc.vector.tensor_copy(out=xsg[h][:], in_=xs[:].indirect(l1[:, 8 * h : 8 * h + 8]))
         for h in range(2):
             nc.vector.tensor_copy(out=xg[h][:], in_=xw[:].indirect(l1[:, 8 * h : 8 * h + 8]))
-        unfold_and_deal(w2s, w2s_raw)
+        nc.vector.tensor_copy(out=w2s_raw[64:128, 0:R].bitcast(I32), in_=w2s_raw[0:64, R : 2 * R].bitcast(I32))
+        deal(w2s, w2s_raw)
         for t in range(PACK):
             nc.scalar.copy(out=w2_t[t][:], in_=w2_raw[:, t : R : PACK])
 
         pa = [ps.tile([P, PACK, HALF], F32, name=f"pa{h}") for h in range(2)]
         pb = [ps.tile([P, PACK, HALF], F32, name=f"pb{h}") for h in range(2)]
         pp = [[ps.tile([P, HALF], F32, name=f"pp{n}{h}") for h in range(2)] for n in range(2)]
-        a_sb = [tile(f"a_sb{h}", [P, HALF, PACK], F32) for h in range(2)]
+        a_sb = tile("a_sb", [P, 2, HALF, PACK], F32, tag="w2_raw")
         for h in range(2):
             for t in range(PACK):
                 nc.tensor.matmul_mx(out=pa[h][:, t, :], lhsT=w_t[t][:].bitcast(E2M1X4),
                                     lhsT_scale=ws[:, P * t : P * (t + 1)],
                                     rhs=xg[h][:].bitcast(E5M2X4), rhs_scale=xsg[h][:], start=True, stop=True)
-            nc.scalar.copy(out=a_sb[h][:], in_=pa[h][:].rearrange("p t j -> p j t"))
+            nc.scalar.copy(out=a_sb[:, h], in_=pa[h][:].rearrange("p t j -> p j t"))
         for h in range(2):
             for t in range(PACK):
                 nc.tensor.matmul_mx(out=pb[h][:, t, :], lhsT=w2_t[t][:].bitcast(E4M3X4),
@@ -135,7 +139,7 @@ def tile_list_outcomegain_kernel(tc, xt_words, xt_scales, w_words, w_scales, w2_
         hs = [tile(f"hs{h}", [P, HALF], U8) for h in range(2)]
         p_sb = [tile(f"p_sb{n}", [P, J], F32) for n in range(2)]
         for h in range(2):
-            nc.vector.tensor_tensor(out=hid[:, h], in0=pb[h][:].rearrange("p t j -> p j t"), in1=a_sb[h][:], op=ALU.max)
+            nc.vector.tensor_tensor(out=hid[:, h], in0=pb[h][:].rearrange("p t j -> p j t"), in1=a_sb[:, h], op=ALU.max)
             nc.vector.quantize_mx(out=hq[h][:].bitcast(E4M3X4), scales=hs[h][:],
                                   in_=hid[:, h].rearrange("p j t -> p (j t)"))
             for n in range(2):

from contextlib import ExitStack

import concourse.mybir as mybir

K, T, J, R, U, V, E, N = 512, 1024, 256, 512, 128, 1024, 512, 256
FLOPS = 2 * K * R * J * 2 + 2 * R * N * J

F32 = mybir.dt.float32
BF16 = mybir.dt.bfloat16
I32 = mybir.dt.int32
U32 = mybir.dt.uint32
U16 = mybir.dt.uint16
U8 = mybir.dt.uint8
FP8 = mybir.dt.float8_e4m3fn
E4M3X4 = mybir.dt.float8_e4m3fn_x4
E5M2X4 = mybir.dt.float8_e5m2_x4
E2M1X4 = mybir.dt.float4_e2m1fn_x4
ALU = mybir.AluOpType
COPY = mybir.ActivationFunctionType.Copy

P = 128
PACK = 4
HALF = 128


def tile_list_outcomegain_kernel(tc, xt_words, xt_scales, w_words, w_scales, w2_words, w2_scales,
                                     wb_words, wb_scales, ca, sz, offs, offs2, offs3, offs4, out):
    nc = tc.nc
    with ExitStack() as ctx:
        sb = ctx.enter_context(tc.tile_pool(name="sb", bufs=1))
        ps = ctx.enter_context(tc.psum_pool(name="ps", bufs=1))

        def tile(name, shape, dtype, tag=None):
            return sb.tile(shape, dtype, name=name, tag=tag or name, align_bytes=64)

        l1 = tile("l1", [P, J // 16], U16)
        l2 = tile("l2", [P, U // 16], U16)
        l3 = tile("l3", [P, U // 16], U16)
        l4 = tile("l4", [P, U // 16], U16)
        xw = tile("xw", [P, T], U32)
        xs = tile("xs", [P, T], U8)
        w_raw = tile("w_raw", [P, 2 * R], U8)
        ws_stage = tile("ws_stage", [4, 4, R // 4], U32)
        ws_raw = tile("ws_raw", [P, R], U8)
        w2_raw = tile("w2_raw", [P, R], U32)
        w2s_raw = tile("w2s_raw", [P, 2 * R], U8)
        wb = tile("wb", [P, 2 * N], U8)
        wbs = tile("wbs", [P, N], U8)
        cat = [tile(f"cat{n}", [P, V], U8) for n in range(2)]
        step = tile("step", [P, 2, 1], F32)
        page = [tile(f"page{n}", [P, E], F32) for n in range(2)]

        nc.vector.memset(xs[:].bitcast(I32), 0)
        nc.vector.memset(ws_raw[:].bitcast(I32), 0)
        nc.vector.memset(w2s_raw[0:64, :].bitcast(I32), 0)
        nc.vector.memset(wbs[:].bitcast(I32), 0)
        for n in range(2):
            nc.vector.memset(page[n][:], 0.0)

        def load_rows(queue, plane, scales, q):
            queue.dma_start(out=plane[32 * q : 32 * q + 4, :].bitcast(I32),
                            in_=scales[0].bitcast(I32)[4 * q : 4 * q + 4, :])

        def load_folded(queue, plane, scales):
            rows = scales[0].bitcast(I32).rearrange("(h q r) c -> q r h c", h=2, q=2)
            for q in range(2):
                queue.dma_start(out=plane[32 * q : 32 * q + 4, :].bitcast(I32).rearrange("p (h c) -> p h c", h=2),
                                in_=rows[q])

        def deal(dealt, plane):
            nc.vector.tensor_copy(out=dealt[:].rearrange("p (t m) -> p t m", t=PACK),
                                  in_=plane[:, 0:R].rearrange("p (m t) -> p t m", t=PACK))

        nc.sync.dma_start(l1[:], offs)
        nc.scalar.dma_start(out=ws_stage[:].bitcast(I32),
                            in_=w_scales[0].bitcast(I32).rearrange("(q r) c -> r q c", q=4))
        nc.scalar.dma_start(out=w_raw[:].bitcast(I32), in_=w_words[0].bitcast(I32))
        for q in range(4):
            load_rows(nc.scalar if q < 2 else nc.sync, xs, xt_scales, q)
        nc.sync.dma_start(out=xw[:].bitcast(I32), in_=xt_words[0].rearrange("p n t -> p (n t)").bitcast(I32))
        nc.sync.dma_start(out=w2_raw[:].bitcast(I32), in_=w2_words[0].rearrange("p n t -> p (n t)").bitcast(I32))
        load_folded(nc.sync, w2s_raw, w2_scales)
        nc.sync.dma_start(l3[:], offs3)
        for n in range(2):
            nc.sync.dma_start(out=cat[n][:], in_=ca[P * n : P * (n + 1), :])
        nc.sync.dma_start(out=wb[:].bitcast(I32), in_=wb_words[0].bitcast(I32))
        for q in range(4):
            load_rows(nc.sync, wbs, wb_scales, q)
        with nc.allow_non_contiguous_dma(reason="one step a partition for each half of the output features"):
            nc.sync.dma_start(out=step[:], in_=sz.rearrange("(h p) o -> p h o", p=P))
        nc.sync.dma_start(l2[:], offs2)
        nc.sync.dma_start(l4[:], offs4)

        w_t = [tile(f"w_t{t}", [P, 2 * P], U8) for t in range(PACK)]
        w2_t = [tile(f"w2_t{t}", [P, P], U32) for t in range(PACK)]
        ws = tile("ws", [P, R], U8)
        w2s = tile("w2s", [P, R], U8)
        xg = [tile(f"xg{h}", [P, HALF], U32) for h in range(2)]
        xsg = [tile(f"xsg{h}", [P, HALF], U8) for h in range(2)]

        for q in range(4):
            nc.vector.tensor_copy(out=ws_raw[32 * q : 32 * q + 4, :].bitcast(U32), in_=ws_stage[:, q, :])
        deal(ws, ws_raw)
        for t in range(PACK):
            nc.scalar.copy(out=w_t[t][:].bitcast(U16), in_=w_raw[:].bitcast(U16)[:, t : R : PACK])
        for h in range(2):
            nc.vector.tensor_copy(out=xsg[h][:], in_=xs[:].indirect(l1[:, 8 * h : 8 * h + 8]))
        for h in range(2):
            nc.vector.tensor_copy(out=xg[h][:], in_=xw[:].indirect(l1[:, 8 * h : 8 * h + 8]))
        nc.vector.tensor_copy(out=w2s_raw[64:128, 0:R].bitcast(I32), in_=w2s_raw[0:64, R : 2 * R].bitcast(I32))
        deal(w2s, w2s_raw)
        for t in range(PACK):
            nc.scalar.copy(out=w2_t[t][:], in_=w2_raw[:, t : R : PACK])

        pa = [ps.tile([P, PACK, HALF], F32, name=f"pa{h}") for h in range(2)]
        pb = [ps.tile([P, PACK, HALF], F32, name=f"pb{h}") for h in range(2)]
        pp = [[ps.tile([P, HALF], F32, name=f"pp{n}{h}") for h in range(2)] for n in range(2)]
        a_sb = tile("a_sb", [P, 2, HALF, PACK], F32, tag="w2_raw")
        for h in range(2):
            for t in range(PACK):
                nc.tensor.matmul_mx(out=pa[h][:, t, :], lhsT=w_t[t][:].bitcast(E2M1X4),
                                    lhsT_scale=ws[:, P * t : P * (t + 1)],
                                    rhs=xg[h][:].bitcast(E5M2X4), rhs_scale=xsg[h][:], start=True, stop=True)
            nc.scalar.copy(out=a_sb[:, h], in_=pa[h][:].rearrange("p t j -> p j t"))
        for h in range(2):
            for t in range(PACK):
                nc.tensor.matmul_mx(out=pb[h][:, t, :], lhsT=w2_t[t][:].bitcast(E4M3X4),
                                    lhsT_scale=w2s[:, P * t : P * (t + 1)],
                                    rhs=xg[h][:].bitcast(E5M2X4), rhs_scale=xsg[h][:], start=True, stop=True)

        cg = [tile(f"cg{n}", [P, U], U8) for n in range(2)]
        gain = [tile(f"gain{n}", [P, U], F32) for n in range(2)]
        for n in range(2):
            nc.vector.tensor_copy(out=cg[n][:], in_=cat[n][:].indirect(l3[:]))
            nc.scalar.activation(out=gain[n][:], in_=cg[n][:].bitcast(FP8), func=COPY, scale=step[:, n, :])

        hid = tile("hid", [P, 2, HALF, PACK], BF16, tag="cat1")
        hq = [tile(f"hq{h}", [P, HALF], U32) for h in range(2)]
        hs = [tile(f"hs{h}", [P, HALF], U8) for h in range(2)]
        p_sb = [tile(f"p_sb{n}", [P, J], F32) for n in range(2)]
        for h in range(2):
            nc.vector.tensor_tensor(out=hid[:, h], in0=pb[h][:].rearrange("p t j -> p j t"), in1=a_sb[:, h], op=ALU.max)
            nc.vector.quantize_mx(out=hq[h][:].bitcast(E4M3X4), scales=hs[h][:],
                                  in_=hid[:, h].rearrange("p j t -> p (j t)"))
            for n in range(2):
                nc.tensor.matmul_mx(out=pp[n][h][:], lhsT=wb[:, 2 * P * n : 2 * P * (n + 1)].bitcast(E2M1X4),
                                    lhsT_scale=wbs[:, P * n : P * (n + 1)],
                                    rhs=hq[h][:].bitcast(E4M3X4), rhs_scale=hs[h][:], start=True, stop=True)
                cols = slice(HALF * h, HALF * (h + 1))
                if n == 1:
                    nc.vector.tensor_copy(out=p_sb[n][:, cols], in_=pp[n][h][:])
                else:
                    nc.scalar.copy(out=p_sb[n][:, cols], in_=pp[n][h][:])

        m0 = tile("m0", [P, U], F32)
        picked = tile("picked", [P, U], F32)
        nc.vector.tensor_tensor(out=m0[:], in0=p_sb[0][:].indirect(l2[:]), in1=gain[0][:], op=ALU.mult)
        nc.scalar.activation(out=picked[:], in_=p_sb[1][:].indirect(l2[:]), func=COPY)
        nc.scalar.activation(out=page[0][:].indirect(l4[:]), in_=m0[:], func=COPY)
        nc.vector.tensor_tensor(out=page[1][:].indirect(l4[:]), in0=picked[:], in1=gain[1][:], op=ALU.mult)
        nc.scalar.dma_start(out=out[0:P, :], in_=page[0][:])
        nc.sync.dma_start(out=out[P : 2 * P, :], in_=page[1][:])
